import numpy as np
import ml_dtypes


def mxq(x, axis, fmt="e4m3"):
    dtype, down = {"e4m3": (ml_dtypes.float8_e4m3fn, 7), "e5m2": (ml_dtypes.float8_e5m2, 14)}[fmt]
    v = np.moveaxis(np.asarray(x, np.float32).astype(ml_dtypes.bfloat16).astype(np.float64), axis, -1)
    blocks = v.reshape(v.shape[:-1] + (-1, 32))
    amax = np.abs(blocks).max(-1, keepdims=True)
    byte = np.maximum(np.where(amax > 0, np.frexp(amax)[1] - 1 + 127, 0) - down, 1)
    scale = np.exp2(byte - 127.0)
    codes = (blocks / scale).astype(np.float32).astype(dtype).astype(np.float64)
    return np.moveaxis((codes * scale).reshape(v.shape), -1, axis)


WIDE = False


def mx_kscale(k):
    if not WIDE:
        return np.ones(k)
    levels = np.array([10, -10, 5, -5, 0])
    if k % 512:
        return np.exp2(np.random.permutation(np.resize(levels, k // 32))).repeat(32)
    a = np.empty((k // 512, 16))
    for p in range(k // 512):
        a[p, :8] = np.random.permutation(np.resize(levels, 8))
        for g in range(8):
            far = levels[np.abs(levels - a[p, g]) >= 10]
            a[p, g + 8] = far[np.random.randint(len(far))]
    return np.exp2(a.ravel()).repeat(32)


def f64(x):
    return np.asarray(x).astype(np.float64)


def striped(idx):
    return np.tile(idx.reshape(-1, 16).T, (8, 1)).astype(np.uint16)


def unstriped(offs):
    return offs[:16].T.reshape(-1).astype(np.int64)


def pack_weight(w):
    k, n = w.shape
    w = f64(np.asarray(w, np.float32).astype(ml_dtypes.bfloat16)).reshape(k // 32, 32, n)
    amax = np.abs(w).max(1)
    byte = np.clip(np.where(amax > 0, np.frexp(amax)[1] - 1 + 127 - 7, 1), 1, 254)
    scaled = (w * np.exp2(127.0 - byte)[:, None, :]).reshape(k, n).astype(np.float32)
    words = np.ascontiguousarray(scaled.reshape(k // 512, 128, 4, n).transpose(0, 1, 3, 2)).astype(ml_dtypes.float8_e4m3fn).view(np.uint8)
    return words, np.ascontiguousarray(byte.astype(np.uint8).reshape(k // 512, 16, n))


def unpack_weight(words, scales):
    g, p, n, _ = words.shape
    vals = np.ascontiguousarray(words).view(ml_dtypes.float8_e4m3fn).astype(np.float64) * np.repeat(np.exp2(scales.astype(np.float64) - 127.0), 8, axis=1)[..., None]
    return vals.transpose(0, 1, 3, 2).reshape(g * 512, n)


K, T, E, C, N = 1024, 512, 8, 128, 128


def by_expert(wq, xq):
    return np.concatenate([wq[e].T @ xq[:, e * C:(e + 1) * C] for e in range(E)], axis=1)


def setup_inputs():
    n = np.random.standard_normal
    s = mx_kscale(K)[:, None]
    first = np.random.permutation(np.repeat(np.arange(E), T // E))
    second = (first + 1 + np.random.permutation(np.repeat(np.arange(E - 1), -(-T // (E - 1)))[:T])) % E
    while np.bincount(second, minlength=E).max() != T // E:
        load = np.bincount(second, minlength=E); hi, lo = int(load.argmax()), int(load.argmin())
        t = np.flatnonzero((second == hi) & (first != lo))[0]; second[t] = lo
    slot_token = np.empty(E * C, np.int64); pos = np.empty((2, T), np.int64); fill = np.zeros(E, np.int64)
    place = np.stack([np.random.permutation(C) for _ in range(E)])
    for r, deal in enumerate((first, second)):
        for t in np.random.permutation(T):
            e = deal[t]; j = e * C + place[e, fill[e]]; fill[e] += 1; slot_token[j] = t; pos[r, t] = j
    g = np.random.uniform(0.2, 0.8, T)
    packed = [pack_weight(m) for m in n((E, K, N)) / np.sqrt(K) / s[None]]
    return {
        "xT": (n((K, T)) * s).astype(np.float32),
        "w_words": np.stack([m[0] for m in packed]),
        "w_scales": np.stack([m[1] for m in packed]),
        "gate": np.stack([np.tile(g, (N, 1)), np.tile(1.0 - g, (N, 1))]).astype(np.float32),
        "offs": striped(slot_token),
        "pos1": striped(pos[0]),
        "pos2": striped(pos[1]),
    }


def reference(xT, w_words, w_scales, gate, offs, pos1, pos2):
    idx = unstriped(offs)
    xq = mxq(f64(xT)[:, idx], 0, "e4m3")
    w = np.stack([unpack_weight(w_words[e], w_scales[e]) for e in range(E)])
    y = by_expert(w, xq)
    return f64(gate[0]) * y[:, unstriped(pos1)] + f64(gate[1]) * y[:, unstriped(pos2)]

@@ -1,0 +1,118 @@
+from contextlib import ExitStack
+
+import concourse.mybir as mybir
+
+K, T, E, C, N = 1024, 512, 8, 128, 128
+SLOTS = E * C
+PASSES = K // 512
+P = 128
+FLOPS = 2 * K * SLOTS * N
+
+F32 = mybir.dt.float32
+BF16 = mybir.dt.bfloat16
+U32 = mybir.dt.uint32
+I32 = mybir.dt.int32
+U16 = mybir.dt.uint16
+U8 = mybir.dt.uint8
+FP8X4 = mybir.dt.float8_e4m3fn_x4
+MULT = mybir.AluOpType.mult
+ADD = mybir.AluOpType.add
+
+WORD_WINDOW = 1408
+BYTE_WINDOW = 1024
+CHUNK = 256
+VECTOR_TOKENS = (176, 0)
+BYTE_CUTS = (0, 512, 896, 1024)
+OUT_CUTS = (0, 256, 512)
+
+
+def tile_routed_moe_kernel(tc, xT, w_words, w_scales, gate, offs, pos1, pos2, out):
+    nc = tc.nc
+    with ExitStack() as ctx:
+        lists = ctx.enter_context(tc.tile_pool(name="lists", bufs=1))
+        keep = ctx.enter_context(tc.tile_pool(name="keep", bufs=1))
+        psum = ctx.enter_context(tc.psum_pool(name="psum", bufs=1))
+
+        offs_sb = lists.tile([P, SLOTS // 16], U16, name="offs_sb")
+        pos1_sb = lists.tile([P, T // 16], U16, name="pos1_sb")
+        pos2_sb = lists.tile([P, T // 16], U16, name="pos2_sb")
+
+        words_all = []
+        for a in range(PASSES):
+            words = keep.tile([P, WORD_WINDOW], U32, name="words_all%d" % a, align_bytes=64)
+            nc.vector.memset(words[:, T:].bitcast(I32), 0)
+            words_all.append(words)
+        bytes_all = keep.tile([P, BYTE_WINDOW], U8, name="bytes_all", align_bytes=64)
+        nc.gpsimd.memset(bytes_all[:], 0)
+        ws = keep.tile([P, E * PASSES, N], U8, name="ws", align_bytes=64)
+        nc.gpsimd.memset(ws[:].rearrange("p b n -> p (b n)").bitcast(I32), 0)
+
+        raw = {}
+        x_view = xT.rearrange("(a p j) t -> a p j t", p=P, j=4)
+        for a in range(PASSES):
+            for c in range(T // CHUNK):
+                chunk = keep.tile([P, 4, CHUNK], F32, name="raw%d_%d" % (a, c))
+                nc.sync.dma_start(out=chunk[:], in_=x_view[a, :, :, c * CHUNK : (c + 1) * CHUNK])
+                raw[a, c] = chunk
+            if a == 0:
+                nc.sync.dma_start(out=offs_sb[:], in_=offs)
+        s_view = w_scales.rearrange("e a q n -> q (e a) n")
+        for q in range(4):
+            nc.sync.dma_start(out=ws[32 * q : 32 * q + 4, :, :].bitcast(I32), in_=s_view[4 * q : 4 * q + 4, :, :].bitcast(I32))
+        ww = keep.tile([P, E * PASSES, 4 * N], U8, name="ww", align_bytes=64)
+        w_view = w_words.rearrange("e a p n r -> p (e a) (n r)")
+        half = E * PASSES // 2
+        for h in range(2):
+            nc.sync.dma_start(out=ww[:, h * half : (h + 1) * half, :], in_=w_view[:, h * half : (h + 1) * half, :])
+        nc.sync.dma_start(out=pos1_sb[:], in_=pos1)
+        nc.sync.dma_start(out=pos2_sb[:], in_=pos2)
+        gates = keep.tile([P, 2, T], F32, name="gates")
+        nc.sync.dma_start(out=gates[:], in_=gate.rearrange("s n t -> n s t"))
+
+        words_slot = keep.tile([P, PASSES, SLOTS], U32, name="words_slot", align_bytes=64)
+        bytes_slot = keep.tile([P, SLOTS], U8, name="bytes_slot", align_bytes=64)
+
+        for a in range(PASSES):
+            grouped = keep.tile([P, T, 4], BF16, name="grouped%d" % a, align_bytes=64)
+            for c in range(T // CHUNK):
+                dst = grouped[:, c * CHUNK : (c + 1) * CHUNK, :].rearrange("p (b i) j -> p b j i", i=4)
+                src = raw[a, c][:].rearrange("p j (b i) -> p b j i", i=4)
+                v = VECTOR_TOKENS[a] // 4
+                if v > 0:
+                    nc.vector.tensor_copy(out=dst[:, :v], in_=src[:, :v])
+                nc.scalar.copy(out=dst[:, v:], in_=src[:, v:])
+            nc.vector.quantize_mx(
+                out=words_all[a][:, :T].bitcast(FP8X4),
+                scales=bytes_all[4 * a :, :T],
+                in_=grouped[:].rearrange("p t j -> p (t j)"),
+            )
+            nc.vector.tensor_copy(out=words_slot[:, a, :], in_=words_all[a][:].indirect(offs_sb[:]))
+
+        y = keep.tile([P, SLOTS], F32, name="y")
+        for b in range(len(BYTE_CUTS) - 1):
+            lo, hi = BYTE_CUTS[b], BYTE_CUTS[b + 1]
+            nc.vector.tensor_copy(out=bytes_slot[:, lo:hi], in_=bytes_all[:].indirect(offs_sb[:, lo // 16 : hi // 16]))
+            sums = psum.tile([N, hi - lo], F32, name="sums%d" % b)
+            for e in range(lo // C, hi // C):
+                cols = slice(e * C, (e + 1) * C)
+                for a in range(PASSES):
+                    nc.tensor.matmul_mx(
+                        out=sums[:, e * C - lo : (e + 1) * C - lo],
+                        lhsT=ww[:, e * PASSES + a, :].bitcast(FP8X4),
+                        lhsT_scale=ws[:, e * PASSES + a, :],
+                        rhs=words_slot[:, a, cols].bitcast(FP8X4),
+                        rhs_scale=bytes_slot[4 * a :, cols],
+                        start=(a == 0),
+                        stop=(a == PASSES - 1),
+                    )
+            nc.scalar.copy(out=y[:, lo:hi], in_=sums[:])
+
+        for b in range(len(OUT_CUTS) - 1):
+            lo, hi = OUT_CUTS[b], OUT_CUTS[b + 1]
+            first = keep.tile([N, hi - lo], F32, name="first%d" % b)
+            second = keep.tile([N, hi - lo], F32, name="second%d" % b)
+            total = keep.tile([N, hi - lo], F32, name="total%d" % b)
+            nc.vector.tensor_tensor(first[:], y[:].indirect(pos1_sb[:, lo // 16 : hi // 16]), gates[:, 0, lo:hi], MULT)
+            nc.vector.tensor_tensor(second[:], y[:].indirect(pos2_sb[:, lo // 16 : hi // 16]), gates[:, 1, lo:hi], MULT)
+            nc.vector.tensor_tensor(total[:], first[:], second[:], ADD)
+            nc.sync.dma_start(out=out[:, lo:hi], in_=total[:])

@@ -20,10 +20,10 @@ ADD = mybir.AluOpType.add
 
 WORD_WINDOW = 1408
 BYTE_WINDOW = 1024
-CHUNK = 256
-VECTOR_TOKENS = (176, 0)
+CHUNKS = (((0, 512, 344),), ((0, 256, 0), (256, 512, 0)))
 BYTE_CUTS = (0, 512, 896, 1024)
-OUT_CUTS = (0, 256, 512)
+BANK_CUTS = ((0, 256, 512), (512, 768, 896), (896, 1024))
+OUT_CUT = 320
 
 
 def tile_routed_moe_kernel(tc, xT, w_words, w_scales, gate, offs, pos1, pos2, out):
@@ -50,10 +50,10 @@ def tile_routed_moe_kernel(tc, xT, w_words, w_scales, gate, offs, pos1, pos2, ou
         raw = {}
         x_view = xT.rearrange("(a p j) t -> a p j t", p=P, j=4)
         for a in range(PASSES):
-            for c in range(T // CHUNK):
-                chunk = keep.tile([P, 4, CHUNK], F32, name="raw%d_%d" % (a, c))
-                nc.sync.dma_start(out=chunk[:], in_=x_view[a, :, :, c * CHUNK : (c + 1) * CHUNK])
-                raw[a, c] = chunk
+            for lo, hi, v in CHUNKS[a]:
+                chunk = keep.tile([P, 4, hi - lo], F32, name="raw%d_%d" % (a, lo))
+                nc.sync.dma_start(out=chunk[:], in_=x_view[a, :, :, lo:hi])
+                raw[a, lo] = chunk
             if a == 0:
                 nc.sync.dma_start(out=offs_sb[:], in_=offs)
         s_view = w_scales.rearrange("e a q n -> q (e a) n")
@@ -74,45 +74,57 @@ def tile_routed_moe_kernel(tc, xT, w_words, w_scales, gate, offs, pos1, pos2, ou
 
         for a in range(PASSES):
             grouped = keep.tile([P, T, 4], BF16, name="grouped%d" % a, align_bytes=64)
-            for c in range(T // CHUNK):
-                dst = grouped[:, c * CHUNK : (c + 1) * CHUNK, :].rearrange("p (b i) j -> p b j i", i=4)
-                src = raw[a, c][:].rearrange("p j (b i) -> p b j i", i=4)
-                v = VECTOR_TOKENS[a] // 4
+            for lo, hi, v in CHUNKS[a]:
+                dst = grouped[:, lo:hi, :].rearrange("p (b i) j -> p b j i", i=4)
+                src = raw[a, lo][:].rearrange("p j (b i) -> p b j i", i=4)
+                nc.scalar.copy(out=dst[:, v // 4 :], in_=src[:, v // 4 :])
                 if v > 0:
-                    nc.vector.tensor_copy(out=dst[:, :v], in_=src[:, :v])
-                nc.scalar.copy(out=dst[:, v:], in_=src[:, v:])
+                    nc.vector.tensor_copy(out=dst[:, : v // 4], in_=src[:, : v // 4])
             nc.vector.quantize_mx(
                 out=words_all[a][:, :T].bitcast(FP8X4),
                 scales=bytes_all[4 * a :, :T],
                 in_=grouped[:].rearrange("p t j -> p (t j)"),
             )
-            nc.vector.tensor_copy(out=words_slot[:, a, :], in_=words_all[a][:].indirect(offs_sb[:]))
+            if a == 0:
+                nc.vector.tensor_copy(out=words_slot[:, a, :], in_=words_all[a][:].indirect(offs_sb[:]))
 
         y = keep.tile([P, SLOTS], F32, name="y")
         for b in range(len(BYTE_CUTS) - 1):
             lo, hi = BYTE_CUTS[b], BYTE_CUTS[b + 1]
+            if b == 1:
+                nc.vector.tensor_copy(out=words_slot[:, 1, 512:], in_=words_all[1][:].indirect(offs_sb[:, 32:]))
             nc.vector.tensor_copy(out=bytes_slot[:, lo:hi], in_=bytes_all[:].indirect(offs_sb[:, lo // 16 : hi // 16]))
-            sums = psum.tile([N, hi - lo], F32, name="sums%d" % b)
-            for e in range(lo // C, hi // C):
-                cols = slice(e * C, (e + 1) * C)
-                for a in range(PASSES):
-                    nc.tensor.matmul_mx(
-                        out=sums[:, e * C - lo : (e + 1) * C - lo],
-                        lhsT=ww[:, e * PASSES + a, :].bitcast(FP8X4),
-                        lhsT_scale=ws[:, e * PASSES + a, :],
-                        rhs=words_slot[:, a, cols].bitcast(FP8X4),
-                        rhs_scale=bytes_slot[4 * a :, cols],
-                        start=(a == 0),
-                        stop=(a == PASSES - 1),
-                    )
-            nc.scalar.copy(out=y[:, lo:hi], in_=sums[:])
+            if b == 0:
+                nc.vector.tensor_copy(out=words_slot[:, 1, :512], in_=words_all[1][:].indirect(offs_sb[:, :32]))
+            for g in range(len(BANK_CUTS[b]) - 1):
+                left, right = BANK_CUTS[b][g], BANK_CUTS[b][g + 1]
+                sums = psum.tile([N, right - left], F32, name="sums%d" % left)
+                for e in range(left // C, right // C):
+                    cols = slice(e * C, (e + 1) * C)
+                    for a in range(PASSES):
+                        nc.tensor.matmul_mx(
+                            out=sums[:, e * C - left : (e + 1) * C - left],
+                            lhsT=ww[:, e * PASSES + a, :].bitcast(FP8X4),
+                            lhsT_scale=ws[:, e * PASSES + a, :],
+                            rhs=words_slot[:, a, cols].bitcast(FP8X4),
+                            rhs_scale=bytes_slot[4 * a :, cols],
+                            start=(a == 0),
+                            stop=(a == PASSES - 1),
+                        )
+                if right == SLOTS:
+                    nc.vector.tensor_copy(out=y[:, left:right], in_=sums[:])
+                else:
+                    nc.scalar.copy(out=y[:, left:right], in_=sums[:])
 
-        for b in range(len(OUT_CUTS) - 1):
-            lo, hi = OUT_CUTS[b], OUT_CUTS[b + 1]
-            first = keep.tile([N, hi - lo], F32, name="first%d" % b)
-            second = keep.tile([N, hi - lo], F32, name="second%d" % b)
-            total = keep.tile([N, hi - lo], F32, name="total%d" % b)
-            nc.vector.tensor_tensor(first[:], y[:].indirect(pos1_sb[:, lo // 16 : hi // 16]), gates[:, 0, lo:hi], MULT)
+        first = keep.tile([N, T], F32, name="first")
+        nc.vector.tensor_tensor(first[:], y[:].indirect(pos1_sb[:]), gates[:, 0, :], MULT)
+        pieces = ((0, OUT_CUT), (OUT_CUT, T))
+        seconds = []
+        for lo, hi in pieces:
+            second = keep.tile([N, hi - lo], F32, name="second%d" % lo)
             nc.vector.tensor_tensor(second[:], y[:].indirect(pos2_sb[:, lo // 16 : hi // 16]), gates[:, 1, lo:hi], MULT)
-            nc.vector.tensor_tensor(total[:], first[:], second[:], ADD)
+            seconds.append(second)
+        for (lo, hi), second in zip(pieces, seconds):
+            total = keep.tile([N, hi - lo], F32, name="total%d" % lo)
+            nc.vector.tensor_tensor(total[:], first[:, lo:hi], second[:], ADD)
             nc.sync.dma_start(out=out[:, lo:hi], in_=total[:])

@@ -18,9 +18,10 @@ FP8X4 = mybir.dt.float8_e4m3fn_x4
 MULT = mybir.AluOpType.mult
 ADD = mybir.AluOpType.add
 
-WORD_WINDOW = 1408
+WORD_WINDOW = 1024
 BYTE_WINDOW = 1024
-CHUNKS = (((0, 512, 344),), ((0, 256, 0), (256, 512, 0)))
+CHUNKS = (((0, 256, 176), (256, 512, 176)), ((0, 256, 0), (256, 512, 0)))
+QUANT_CUTS = ((0, 256, 512), (0, 512))
 BYTE_CUTS = (0, 512, 896, 1024)
 BANK_CUTS = ((0, 256, 512), (512, 768, 896), (896, 1024))
 OUT_CUT = 320
@@ -43,7 +44,7 @@ def tile_routed_moe_kernel(tc, xT, w_words, w_scales, gate, offs, pos1, pos2, ou
             nc.vector.memset(words[:, T:].bitcast(I32), 0)
             words_all.append(words)
         bytes_all = keep.tile([P, BYTE_WINDOW], U8, name="bytes_all", align_bytes=64)
-        nc.gpsimd.memset(bytes_all[:], 0)
+        nc.gpsimd.memset(bytes_all[:].bitcast(I32), 0)
         ws = keep.tile([P, E * PASSES, N], U8, name="ws", align_bytes=64)
         nc.gpsimd.memset(ws[:].rearrange("p b n -> p (b n)").bitcast(I32), 0)
 
@@ -80,13 +81,16 @@ def tile_routed_moe_kernel(tc, xT, w_words, w_scales, gate, offs, pos1, pos2, ou
                 nc.scalar.copy(out=dst[:, v // 4 :], in_=src[:, v // 4 :])
                 if v > 0:
                     nc.vector.tensor_copy(out=dst[:, : v // 4], in_=src[:, : v // 4])
-            nc.vector.quantize_mx(
-                out=words_all[a][:, :T].bitcast(FP8X4),
-                scales=bytes_all[4 * a :, :T],
-                in_=grouped[:].rearrange("p t j -> p (t j)"),
-            )
+                if hi in QUANT_CUTS[a]:
+                    cut = QUANT_CUTS[a][list(QUANT_CUTS[a]).index(hi) - 1]
+                    nc.vector.quantize_mx(
+                        out=words_all[a][:, cut:hi].bitcast(FP8X4),
+                        scales=bytes_all[4 * a :, cut:hi],
+                        in_=grouped[:, cut:hi, :].rearrange("p t j -> p (t j)"),
+                    )
             if a == 0:
-                nc.vector.tensor_copy(out=words_slot[:, a, :], in_=words_all[a][:].indirect(offs_sb[:]))
+                nc.vector.tensor_copy(out=words_slot[:, 0, :768], in_=words_all[0][:].indirect(offs_sb[:, :48]))
+        nc.vector.tensor_copy(out=words_slot[:, 0, 768:], in_=words_all[0][:].indirect(offs_sb[:, 48:]))
 
         y = keep.tile([P, SLOTS], F32, name="y")
         for b in range(len(BYTE_CUTS) - 1):

from contextlib import ExitStack

import concourse.mybir as mybir

K, T, E, C, N = 1024, 512, 8, 128, 128
SLOTS = E * C
PASSES = K // 512
P = 128
FLOPS = 2 * K * SLOTS * N

F32 = mybir.dt.float32
BF16 = mybir.dt.bfloat16
U32 = mybir.dt.uint32
I32 = mybir.dt.int32
U16 = mybir.dt.uint16
U8 = mybir.dt.uint8
FP8X4 = mybir.dt.float8_e4m3fn_x4
MULT = mybir.AluOpType.mult
ADD = mybir.AluOpType.add

WORD_WINDOW = 1024
BYTE_WINDOW = 1024
CHUNKS = (((0, 256, 176), (256, 512, 176)), ((0, 256, 0), (256, 512, 0)))
QUANT_CUTS = ((0, 256, 512), (0, 512))
BYTE_CUTS = (0, 512, 896, 1024)
BANK_CUTS = ((0, 256, 512), (512, 768, 896), (896, 1024))
OUT_CUT = 320


def tile_routed_moe_kernel(tc, xT, w_words, w_scales, gate, offs, pos1, pos2, out):
    nc = tc.nc
    with ExitStack() as ctx:
        lists = ctx.enter_context(tc.tile_pool(name="lists", bufs=1))
        keep = ctx.enter_context(tc.tile_pool(name="keep", bufs=1))
        psum = ctx.enter_context(tc.psum_pool(name="psum", bufs=1))

        offs_sb = lists.tile([P, SLOTS // 16], U16, name="offs_sb")
        pos1_sb = lists.tile([P, T // 16], U16, name="pos1_sb")
        pos2_sb = lists.tile([P, T // 16], U16, name="pos2_sb")

        words_all = []
        for a in range(PASSES):
            words = keep.tile([P, WORD_WINDOW], U32, name="words_all%d" % a, align_bytes=64)
            nc.vector.memset(words[:, T:].bitcast(I32), 0)
            words_all.append(words)
        bytes_all = keep.tile([P, BYTE_WINDOW], U8, name="bytes_all", align_bytes=64)
        nc.gpsimd.memset(bytes_all[:].bitcast(I32), 0)
        ws = keep.tile([P, E * PASSES, N], U8, name="ws", align_bytes=64)
        nc.gpsimd.memset(ws[:].rearrange("p b n -> p (b n)").bitcast(I32), 0)

        raw = {}
        x_view = xT.rearrange("(a p j) t -> a p j t", p=P, j=4)
        for a in range(PASSES):
            for lo, hi, v in CHUNKS[a]:
                chunk = keep.tile([P, 4, hi - lo], F32, name="raw%d_%d" % (a, lo))
                nc.sync.dma_start(out=chunk[:], in_=x_view[a, :, :, lo:hi])
                raw[a, lo] = chunk
            if a == 0:
                nc.sync.dma_start(out=offs_sb[:], in_=offs)
        s_view = w_scales.rearrange("e a q n -> q (e a) n")
        for q in range(4):
            nc.sync.dma_start(out=ws[32 * q : 32 * q + 4, :, :].bitcast(I32), in_=s_view[4 * q : 4 * q + 4, :, :].bitcast(I32))
        ww = keep.tile([P, E * PASSES, 4 * N], U8, name="ww", align_bytes=64)
        w_view = w_words.rearrange("e a p n r -> p (e a) (n r)")
        half = E * PASSES // 2
        for h in range(2):
            nc.sync.dma_start(out=ww[:, h * half : (h + 1) * half, :], in_=w_view[:, h * half : (h + 1) * half, :])
        nc.sync.dma_start(out=pos1_sb[:], in_=pos1)
        nc.sync.dma_start(out=pos2_sb[:], in_=pos2)
        gates = keep.tile([P, 2, T], F32, name="gates")
        nc.sync.dma_start(out=gates[:], in_=gate.rearrange("s n t -> n s t"))

        words_slot = keep.tile([P, PASSES, SLOTS], U32, name="words_slot", align_bytes=64)
        bytes_slot = keep.tile([P, SLOTS], U8, name="bytes_slot", align_bytes=64)

        for a in range(PASSES):
            grouped = keep.tile([P, T, 4], BF16, name="grouped%d" % a, align_bytes=64)
            for lo, hi, v in CHUNKS[a]:
                dst = grouped[:, lo:hi, :].rearrange("p (b i) j -> p b j i", i=4)
                src = raw[a, lo][:].rearrange("p j (b i) -> p b j i", i=4)
                nc.scalar.copy(out=dst[:, v // 4 :], in_=src[:, v // 4 :])
                if v > 0:
                    nc.vector.tensor_copy(out=dst[:, : v // 4], in_=src[:, : v // 4])
                if hi in QUANT_CUTS[a]:
                    cut = QUANT_CUTS[a][list(QUANT_CUTS[a]).index(hi) - 1]
                    nc.vector.quantize_mx(
                        out=words_all[a][:, cut:hi].bitcast(FP8X4),
                        scales=bytes_all[4 * a :, cut:hi],
                        in_=grouped[:, cut:hi, :].rearrange("p t j -> p (t j)"),
                    )
            if a == 0:
                nc.vector.tensor_copy(out=words_slot[:, 0, :768], in_=words_all[0][:].indirect(offs_sb[:, :48]))
        nc.vector.tensor_copy(out=words_slot[:, 0, 768:], in_=words_all[0][:].indirect(offs_sb[:, 48:]))

        y = keep.tile([P, SLOTS], F32, name="y")
        for b in range(len(BYTE_CUTS) - 1):
            lo, hi = BYTE_CUTS[b], BYTE_CUTS[b + 1]
            if b == 1:
                nc.vector.tensor_copy(out=words_slot[:, 1, 512:], in_=words_all[1][:].indirect(offs_sb[:, 32:]))
            nc.vector.tensor_copy(out=bytes_slot[:, lo:hi], in_=bytes_all[:].indirect(offs_sb[:, lo // 16 : hi // 16]))
            if b == 0:
                nc.vector.tensor_copy(out=words_slot[:, 1, :512], in_=words_all[1][:].indirect(offs_sb[:, :32]))
            for g in range(len(BANK_CUTS[b]) - 1):
                left, right = BANK_CUTS[b][g], BANK_CUTS[b][g + 1]
                sums = psum.tile([N, right - left], F32, name="sums%d" % left)
                for e in range(left // C, right // C):
                    cols = slice(e * C, (e + 1) * C)
                    for a in range(PASSES):
                        nc.tensor.matmul_mx(
                            out=sums[:, e * C - left : (e + 1) * C - left],
                            lhsT=ww[:, e * PASSES + a, :].bitcast(FP8X4),
                            lhsT_scale=ws[:, e * PASSES + a, :],
                            rhs=words_slot[:, a, cols].bitcast(FP8X4),
                            rhs_scale=bytes_slot[4 * a :, cols],
                            start=(a == 0),
                            stop=(a == PASSES - 1),
                        )
                if right == SLOTS:
                    nc.vector.tensor_copy(out=y[:, left:right], in_=sums[:])
                else:
                    nc.scalar.copy(out=y[:, left:right], in_=sums[:])

        first = keep.tile([N, T], F32, name="first")
        nc.vector.tensor_tensor(first[:], y[:].indirect(pos1_sb[:]), gates[:, 0, :], MULT)
        pieces = ((0, OUT_CUT), (OUT_CUT, T))
        seconds = []
        for lo, hi in pieces:
            second = keep.tile([N, hi - lo], F32, name="second%d" % lo)
            nc.vector.tensor_tensor(second[:], y[:].indirect(pos2_sb[:, lo // 16 : hi // 16]), gates[:, 1, lo:hi], MULT)
            seconds.append(second)
        for (lo, hi), second in zip(pieces, seconds):
            total = keep.tile([N, hi - lo], F32, name="total%d" % lo)
            nc.vector.tensor_tensor(total[:], first[:, lo:hi], second[:], ADD)
            nc.sync.dma_start(out=out[:, lo:hi], in_=total[:])
